import numpy as np
CORES = [144,145,146,147,148,149,150,151,272,273,274,275,276,277,278,279]
N = 16
ROOT = 12
def setup_inputs(rng):
    return {"x": rng.standard_normal((N, 128, 1024), dtype=np.float32)}
def reference(x):
    y = np.full(x.shape, np.nan, x.dtype)
    y[ROOT] = x.sum(axis=0, dtype=np.float64).astype(x.dtype)
    return {"y": y}

@@ -1,0 +1,93 @@
+from concourse.bass import DstId, RemoteDMATransfer
+from concourse.mybir import AluOpType
+
+SCRATCH = {
+    "xs": ("dram", [8, 128, 128], "float32"),
+    "rs": ("dram", [7, 128, 128], "float32"),
+    "xa": ("dram", [5, 128, 144], "float32"),
+    "xb": ("dram", [2, 128, 152], "float32"),
+    "ra": ("dram", [7, 128, 144], "float32"),
+    "rb": ("dram", [7, 128, 152], "float32"),
+}
+SEMAPHORES = ["lda", "ldb", "arr", "sent", "gota", "gotb", "gotfar", "stored", "done"]
+
+NA, NB = 5, 2
+ROWS_A = 18 * NA
+
+
+def rank_program(g, core, T, topo):
+    rank = T.rank_of(core)
+    if rank is None:
+        return
+    sem = T.sem
+    root = T.cores[T.root]
+    far = [c for c in T.cores if topo.host(c) != topo.host(root)]
+    near = [c for c in T.cores if topo.host(c) == topo.host(root)]
+    owners = [c for c in near if c != root]
+
+    def to(dst):
+        rid, pid = topo.addr(dst, core)
+        return [DstId(rid=rid, pnc=pid)]
+
+    def slot(sender, receiver, chip_cores):
+        return [c for c in chip_cores if c != receiver].index(sender)
+
+    if core in far:
+        me = far.index(core)
+        g.sync.dma_start(T.xs[:], T.x[:]).then_inc(sem.lda, 16)
+        g.wait_ge(sem.lda, 16)
+        spread = []
+        for d, dst in enumerate(far):
+            if dst == core:
+                continue
+            spread.append(RemoteDMATransfer(dst_ids=to(dst), dma_engine_mask=3 << (2 * len(spread)), remote_sem=sem.arr,
+                                            src=T.xs[d], dst=T.rs[slot(core, dst, far)]))
+        g.remote_dma_fused(spread, local_sem=sem.sent)
+        g.wait_ge(sem.arr, 14)
+        g.remote_dma_fused([RemoteDMATransfer(dst_ids=to(root), dma_engine_mask=0xFF, remote_sem=sem.gotfar,
+                                              srcs=[T.xs[me]] + [T.rs[s] for s in range(7)], dsts=[T.xs[me]], alu_op=1)],
+                           local_sem=sem.sent)
+        g.wait_ge(sem.sent, 14 + 8)
+        return
+
+    g.scalar.dma_start(T.xb[:], T.x[ROWS_A:128, :]).then_inc(sem.ldb, 16)
+    g.sync.dma_start(T.xa[:], T.x[0:ROWS_A, :]).then_inc(sem.lda, 16)
+    call_a, call_b = [], []
+    for p, dst in enumerate(owners):
+        if dst == core:
+            continue
+        s = slot(core, dst, near)
+        if p < NA:
+            call_a.append(RemoteDMATransfer(dst_ids=to(dst), dma_engine_mask=3 << (2 * p), remote_sem=sem.arr,
+                                            src=T.xa[p], dst=T.ra[s]))
+        else:
+            call_b.append(RemoteDMATransfer(dst_ids=to(dst), dma_engine_mask=3 << (2 * p), remote_sem=sem.arr,
+                                            src=T.xb[p - NA], dst=T.rb[s]))
+    g.wait_ge(sem.ldb, 16)
+    g.remote_dma_fused(call_b, local_sem=sem.sent)
+    g.wait_ge(sem.lda, 16)
+    g.remote_dma_fused(call_a, local_sem=sem.sent)
+    n_sent = 2 * (len(call_a) + len(call_b))
+
+    if core != root:
+        p = owners.index(core)
+        g.wait_ge(sem.arr, 14)
+        if p < NA:
+            fold = RemoteDMATransfer(dst_ids=to(root), dma_engine_mask=0xFFFF, remote_sem=sem.gota,
+                                     srcs=[T.xa[p]] + [T.ra[s] for s in range(7)], dsts=[T.ra[p]], alu_op=1)
+        else:
+            fold = RemoteDMATransfer(dst_ids=to(root), dma_engine_mask=0xFFFF, remote_sem=sem.gotb,
+                                     srcs=[T.xb[p - NA]] + [T.rb[s] for s in range(7)], dsts=[T.rb[p - NA]], alu_op=1)
+        g.remote_dma_fused([fold], local_sem=sem.sent)
+        g.wait_ge(sem.sent, n_sent + 16)
+        return
+
+    g.sync.wait_ge(sem.gota, 16 * NA)
+    g.sync.dma_start(T.y[0:ROWS_A, :], T.ra[0:NA]).then_inc(sem.stored, 16)
+    g.scalar.wait_ge(sem.gotb, 16 * NB)
+    g.scalar.dma_start(T.y[ROWS_A:128, :], T.rb[0:NB]).then_inc(sem.stored, 16)
+    g.wait_ge(sem.sent, n_sent)
+    g.wait_ge(sem.stored, 32)
+    g.wait_ge(sem.gotfar, 8 * 8)
+    g.dma_start(T.y[:], T.xs[:], accum_op=AluOpType.add, max_dma_last_dim=8192).then_inc(sem.done, 16)
+    g.wait_ge(sem.done, 16)

@@ -1,15 +1,20 @@
 from concourse.bass import DstId, RemoteDMATransfer
 from concourse.mybir import AluOpType
 
+K = 2
+W = 128 // K
+CR = 128 // K
+
 SCRATCH = {
-    "xs": ("dram", [8, 128, 128], "float32"),
-    "rs": ("dram", [7, 128, 128], "float32"),
+    "xs": ("dram", [8 * K, 128, W], "float32"),
+    "rs": ("dram", [7 * K, 128, W], "float32"),
     "xa": ("dram", [5, 128, 144], "float32"),
     "xb": ("dram", [2, 128, 152], "float32"),
     "ra": ("dram", [7, 128, 144], "float32"),
     "rb": ("dram", [7, 128, 152], "float32"),
 }
-SEMAPHORES = ["lda", "ldb", "arr", "sent", "gota", "gotb", "gotfar", "stored", "done"]
+SEMAPHORES = (["lda", "ldb", "arr", "sent", "gota", "gotb", "stored", "done"]
+              + ["ld%d" % c for c in range(K)] + ["arr%d" % c for c in range(K)] + ["far%d" % c for c in range(K)])
 
 NA, NB = 5, 2
 ROWS_A = 18 * NA
@@ -34,20 +39,26 @@ def rank_program(g, core, T, topo):
 
     if core in far:
         me = far.index(core)
-        g.sync.dma_start(T.xs[:], T.x[:]).then_inc(sem.lda, 16)
-        g.wait_ge(sem.lda, 16)
-        spread = []
-        for d, dst in enumerate(far):
-            if dst == core:
-                continue
-            spread.append(RemoteDMATransfer(dst_ids=to(dst), dma_engine_mask=3 << (2 * len(spread)), remote_sem=sem.arr,
-                                            src=T.xs[d], dst=T.rs[slot(core, dst, far)]))
-        g.remote_dma_fused(spread, local_sem=sem.sent)
-        g.wait_ge(sem.arr, 14)
-        g.remote_dma_fused([RemoteDMATransfer(dst_ids=to(root), dma_engine_mask=0xFF, remote_sem=sem.gotfar,
-                                              srcs=[T.xs[me]] + [T.rs[s] for s in range(7)], dsts=[T.xs[me]], alu_op=1)],
-                           local_sem=sem.sent)
-        g.wait_ge(sem.sent, 14 + 8)
+        for c in range(K):
+            q = g.sync if c % 2 == 0 else g.scalar
+            q.dma_start(T.xs[8 * c:8 * c + 8], T.x[CR * c:CR * (c + 1), :]).then_inc(sem["ld%d" % c], 16)
+        for c in range(K):
+            g.wait_ge(sem["ld%d" % c], 16)
+            spread = []
+            for d, dst in enumerate(far):
+                if dst == core:
+                    continue
+                spread.append(RemoteDMATransfer(dst_ids=to(dst), dma_engine_mask=3 << (2 * len(spread)),
+                                                remote_sem=sem["arr%d" % c], src=T.xs[8 * c + d],
+                                                dst=T.rs[7 * c + slot(core, dst, far)]))
+            g.remote_dma_fused(spread, local_sem=sem.sent)
+        for c in range(K):
+            g.wait_ge(sem["arr%d" % c], 14)
+            g.remote_dma_fused([RemoteDMATransfer(dst_ids=to(root), dma_engine_mask=0xFF, remote_sem=sem["far%d" % c],
+                                                  srcs=[T.xs[8 * c + me]] + [T.rs[7 * c + s] for s in range(7)],
+                                                  dsts=[T.xs[8 * c + me]], alu_op=1)],
+                               local_sem=sem.sent)
+        g.wait_ge(sem.sent, K * (14 + 8))
         return
 
     g.scalar.dma_start(T.xb[:], T.x[ROWS_A:128, :]).then_inc(sem.ldb, 16)
@@ -88,6 +99,8 @@ def rank_program(g, core, T, topo):
     g.scalar.dma_start(T.y[ROWS_A:128, :], T.rb[0:NB]).then_inc(sem.stored, 16)
     g.wait_ge(sem.sent, n_sent)
     g.wait_ge(sem.stored, 32)
-    g.wait_ge(sem.gotfar, 8 * 8)
-    g.dma_start(T.y[:], T.xs[:], accum_op=AluOpType.add, max_dma_last_dim=8192).then_inc(sem.done, 16)
-    g.wait_ge(sem.done, 16)
+    for c in range(K):
+        g.wait_ge(sem["far%d" % c], 8 * 8)
+        g.dma_start(T.y[CR * c:CR * (c + 1), :], T.xs[8 * c:8 * c + 8], accum_op=AluOpType.add,
+                    max_dma_last_dim=8192).then_inc(sem.done, 16)
+    g.wait_ge(sem.done, 16 * K)

@@ -1,23 +1,19 @@
 from concourse.bass import DstId, RemoteDMATransfer
 from concourse.mybir import AluOpType
 
-K = 2
-W = 128 // K
-CR = 128 // K
+ROWS = [32, 48, 48]
+K = len(ROWS)
+OFF = [sum(ROWS[:c]) for c in range(K + 1)]
 
-SCRATCH = {
-    "xs": ("dram", [8 * K, 128, W], "float32"),
-    "rs": ("dram", [7 * K, 128, W], "float32"),
-    "xa": ("dram", [5, 128, 144], "float32"),
-    "xb": ("dram", [2, 128, 152], "float32"),
-    "ra": ("dram", [7, 128, 144], "float32"),
-    "rb": ("dram", [7, 128, 152], "float32"),
-}
-SEMAPHORES = (["lda", "ldb", "arr", "sent", "gota", "gotb", "stored", "done"]
-              + ["ld%d" % c for c in range(K)] + ["arr%d" % c for c in range(K)] + ["far%d" % c for c in range(K)])
-
-NA, NB = 5, 2
-ROWS_A = 18 * NA
+SCRATCH = {}
+for _c in range(K):
+    SCRATCH["xs%d" % _c] = ("dram", [8, 128, ROWS[_c]], "float32")
+    SCRATCH["rs%d" % _c] = ("dram", [7, 128, ROWS[_c]], "float32")
+    SCRATCH["rx%d" % _c] = ("dram", [7, 128, ROWS[_c]], "float32")
+    SCRATCH["ln%d" % _c] = ("dram", [8, 128, ROWS[_c]], "float32")
+    SCRATCH["lf%d" % _c] = ("dram", [8, 128, ROWS[_c]], "float32")
+SEMAPHORES = (["sent", "done"] + ["ld%d" % c for c in range(K)] + ["arr%d" % c for c in range(K)]
+              + ["far%d" % c for c in range(K)] + ["near%d" % c for c in range(K)] + ["st%d" % c for c in range(K)])
 
 
 def rank_program(g, core, T, topo):
@@ -26,81 +22,67 @@ def rank_program(g, core, T, topo):
         return
     sem = T.sem
     root = T.cores[T.root]
-    far = [c for c in T.cores if topo.host(c) != topo.host(root)]
-    near = [c for c in T.cores if topo.host(c) == topo.host(root)]
-    owners = [c for c in near if c != root]
+    is_far = topo.host(core) != topo.host(root)
+    chip = [c for c in T.cores if topo.host(c) == topo.host(core)]
+    if is_far:
+        def owner(c, d):
+            return chip[d]
+    else:
+        others = [c for c in chip if c != root]
+        neigh = [c for c in others if topo.die(c) == topo.die(root)]
+
+        def owner(c, d):
+            return others[d] if d < 7 else neigh[c % len(neigh)]
 
     def to(dst):
         rid, pid = topo.addr(dst, core)
         return [DstId(rid=rid, pnc=pid)]
 
-    def slot(sender, receiver, chip_cores):
-        return [c for c in chip_cores if c != receiver].index(sender)
+    def queue(c):
+        return g.sync if c % 2 == 0 else g.scalar
 
-    if core in far:
-        me = far.index(core)
-        for c in range(K):
-            q = g.sync if c % 2 == 0 else g.scalar
-            q.dma_start(T.xs[8 * c:8 * c + 8], T.x[CR * c:CR * (c + 1), :]).then_inc(sem["ld%d" % c], 16)
-        for c in range(K):
-            g.wait_ge(sem["ld%d" % c], 16)
-            spread = []
-            for d, dst in enumerate(far):
-                if dst == core:
-                    continue
-                spread.append(RemoteDMATransfer(dst_ids=to(dst), dma_engine_mask=3 << (2 * len(spread)),
-                                                remote_sem=sem["arr%d" % c], src=T.xs[8 * c + d],
-                                                dst=T.rs[7 * c + slot(core, dst, far)]))
-            g.remote_dma_fused(spread, local_sem=sem.sent)
-        for c in range(K):
-            g.wait_ge(sem["arr%d" % c], 14)
-            g.remote_dma_fused([RemoteDMATransfer(dst_ids=to(root), dma_engine_mask=0xFF, remote_sem=sem["far%d" % c],
-                                                  srcs=[T.xs[8 * c + me]] + [T.rs[7 * c + s] for s in range(7)],
-                                                  dsts=[T.xs[8 * c + me]], alu_op=1)],
-                               local_sem=sem.sent)
-        g.wait_ge(sem.sent, K * (14 + 8))
-        return
+    def landed(c, d):
+        return T[("rs%d" if (is_far or d < 7) else "rx%d") % c]
 
-    g.scalar.dma_start(T.xb[:], T.x[ROWS_A:128, :]).then_inc(sem.ldb, 16)
-    g.sync.dma_start(T.xa[:], T.x[0:ROWS_A, :]).then_inc(sem.lda, 16)
-    call_a, call_b = [], []
-    for p, dst in enumerate(owners):
-        if dst == core:
-            continue
-        s = slot(core, dst, near)
-        if p < NA:
-            call_a.append(RemoteDMATransfer(dst_ids=to(dst), dma_engine_mask=3 << (2 * p), remote_sem=sem.arr,
-                                            src=T.xa[p], dst=T.ra[s]))
-        else:
-            call_b.append(RemoteDMATransfer(dst_ids=to(dst), dma_engine_mask=3 << (2 * p), remote_sem=sem.arr,
-                                            src=T.xb[p - NA], dst=T.rb[s]))
-    g.wait_ge(sem.ldb, 16)
-    g.remote_dma_fused(call_b, local_sem=sem.sent)
-    g.wait_ge(sem.lda, 16)
-    g.remote_dma_fused(call_a, local_sem=sem.sent)
-    n_sent = 2 * (len(call_a) + len(call_b))
+    n_sent = 0
+    for c in range(K):
+        queue(c).dma_start(T["xs%d" % c][:], T.x[OFF[c]:OFF[c + 1], :]).then_inc(sem["ld%d" % c], 16)
+    for c in range(K):
+        g.wait_ge(sem["ld%d" % c], 16)
+        spread = []
+        for d in range(8):
+            dst = owner(c, d)
+            if dst == core:
+                continue
+            s = [k for k in chip if k != dst].index(core)
+            spread.append(RemoteDMATransfer(dst_ids=to(dst), dma_engine_mask=3 << (2 * d), remote_sem=sem["arr%d" % c],
+                                            src=T["xs%d" % c][d], dst=landed(c, d)[s]))
+        g.remote_dma_fused(spread, local_sem=sem.sent)
+        n_sent += 2 * len(spread)
 
     if core != root:
-        p = owners.index(core)
-        g.wait_ge(sem.arr, 14)
-        if p < NA:
-            fold = RemoteDMATransfer(dst_ids=to(root), dma_engine_mask=0xFFFF, remote_sem=sem.gota,
-                                     srcs=[T.xa[p]] + [T.ra[s] for s in range(7)], dsts=[T.ra[p]], alu_op=1)
-        else:
-            fold = RemoteDMATransfer(dst_ids=to(root), dma_engine_mask=0xFFFF, remote_sem=sem.gotb,
-                                     srcs=[T.xb[p - NA]] + [T.rb[s] for s in range(7)], dsts=[T.rb[p - NA]], alu_op=1)
-        g.remote_dma_fused([fold], local_sem=sem.sent)
-        g.wait_ge(sem.sent, n_sent + 16)
+        for c in range(K):
+            mine = [d for d in range(8) if owner(c, d) == core]
+            g.wait_ge(sem["arr%d" % c], 14 * len(mine))
+            n_eng = (8 if is_far else 16) // len(mine)
+            folds = []
+            for i, d in enumerate(mine):
+                folds.append(RemoteDMATransfer(dst_ids=to(root), dma_engine_mask=((1 << n_eng) - 1) << (n_eng * i),
+                                               remote_sem=sem[("far%d" if is_far else "near%d") % c],
+                                               srcs=[T["xs%d" % c][d]] + [landed(c, d)[s] for s in range(7)],
+                                               dsts=[T[("lf%d" if is_far else "ln%d") % c][d]], alu_op=1))
+            g.remote_dma_fused(folds, local_sem=sem.sent)
+            n_sent += n_eng * len(mine)
+        g.wait_ge(sem.sent, n_sent)
         return
 
-    g.sync.wait_ge(sem.gota, 16 * NA)
-    g.sync.dma_start(T.y[0:ROWS_A, :], T.ra[0:NA]).then_inc(sem.stored, 16)
-    g.scalar.wait_ge(sem.gotb, 16 * NB)
-    g.scalar.dma_start(T.y[ROWS_A:128, :], T.rb[0:NB]).then_inc(sem.stored, 16)
-    g.wait_ge(sem.sent, n_sent)
-    g.wait_ge(sem.stored, 32)
     for c in range(K):
+        queue(c).wait_ge(sem["near%d" % c], 7 * 16)
+        queue(c).dma_start(T.y[OFF[c]:OFF[c + 1], :], T["ln%d" % c][:]).then_inc(sem["st%d" % c], 16)
+    for c in range(K):
+        g.wait_ge(sem["st%d" % c], 16)
         g.wait_ge(sem["far%d" % c], 8 * 8)
-        g.dma_start(T.y[CR * c:CR * (c + 1), :], T.xs[8 * c:8 * c + 8], accum_op=AluOpType.add,
+        g.dma_start(T.y[OFF[c]:OFF[c + 1], :], T["lf%d" % c][:], accum_op=AluOpType.add,
                     max_dma_last_dim=8192).then_inc(sem.done, 16)
     g.wait_ge(sem.done, 16 * K)
+    g.wait_ge(sem.sent, n_sent)

from concourse.bass import DstId, RemoteDMATransfer
from concourse.mybir import AluOpType

ROWS = [32, 48, 48]
K = len(ROWS)
OFF = [sum(ROWS[:c]) for c in range(K + 1)]

SCRATCH = {}
for _c in range(K):
    SCRATCH["xs%d" % _c] = ("dram", [8, 128, ROWS[_c]], "float32")
    SCRATCH["rs%d" % _c] = ("dram", [7, 128, ROWS[_c]], "float32")
    SCRATCH["rx%d" % _c] = ("dram", [7, 128, ROWS[_c]], "float32")
    SCRATCH["ln%d" % _c] = ("dram", [8, 128, ROWS[_c]], "float32")
    SCRATCH["lf%d" % _c] = ("dram", [8, 128, ROWS[_c]], "float32")
SEMAPHORES = (["sent", "done"] + ["ld%d" % c for c in range(K)] + ["arr%d" % c for c in range(K)]
              + ["far%d" % c for c in range(K)] + ["near%d" % c for c in range(K)] + ["st%d" % c for c in range(K)])


def rank_program(g, core, T, topo):
    rank = T.rank_of(core)
    if rank is None:
        return
    sem = T.sem
    root = T.cores[T.root]
    is_far = topo.host(core) != topo.host(root)
    chip = [c for c in T.cores if topo.host(c) == topo.host(core)]
    if is_far:
        def owner(c, d):
            return chip[d]
    else:
        others = [c for c in chip if c != root]
        neigh = [c for c in others if topo.die(c) == topo.die(root)]

        def owner(c, d):
            return others[d] if d < 7 else neigh[c % len(neigh)]

    def to(dst):
        rid, pid = topo.addr(dst, core)
        return [DstId(rid=rid, pnc=pid)]

    def queue(c):
        return g.sync if c % 2 == 0 else g.scalar

    def landed(c, d):
        return T[("rs%d" if (is_far or d < 7) else "rx%d") % c]

    n_sent = 0
    for c in range(K):
        queue(c).dma_start(T["xs%d" % c][:], T.x[OFF[c]:OFF[c + 1], :]).then_inc(sem["ld%d" % c], 16)
    for c in range(K):
        g.wait_ge(sem["ld%d" % c], 16)
        spread = []
        for d in range(8):
            dst = owner(c, d)
            if dst == core:
                continue
            s = [k for k in chip if k != dst].index(core)
            spread.append(RemoteDMATransfer(dst_ids=to(dst), dma_engine_mask=3 << (2 * d), remote_sem=sem["arr%d" % c],
                                            src=T["xs%d" % c][d], dst=landed(c, d)[s]))
        g.remote_dma_fused(spread, local_sem=sem.sent)
        n_sent += 2 * len(spread)

    if core != root:
        for c in range(K):
            mine = [d for d in range(8) if owner(c, d) == core]
            g.wait_ge(sem["arr%d" % c], 14 * len(mine))
            n_eng = (8 if is_far else 16) // len(mine)
            folds = []
            for i, d in enumerate(mine):
                folds.append(RemoteDMATransfer(dst_ids=to(root), dma_engine_mask=((1 << n_eng) - 1) << (n_eng * i),
                                               remote_sem=sem[("far%d" if is_far else "near%d") % c],
                                               srcs=[T["xs%d" % c][d]] + [landed(c, d)[s] for s in range(7)],
                                               dsts=[T[("lf%d" if is_far else "ln%d") % c][d]], alu_op=1))
            g.remote_dma_fused(folds, local_sem=sem.sent)
            n_sent += n_eng * len(mine)
        g.wait_ge(sem.sent, n_sent)
        return

    for c in range(K):
        queue(c).wait_ge(sem["near%d" % c], 7 * 16)
        queue(c).dma_start(T.y[OFF[c]:OFF[c + 1], :], T["ln%d" % c][:]).then_inc(sem["st%d" % c], 16)
    for c in range(K):
        g.wait_ge(sem["st%d" % c], 16)
        g.wait_ge(sem["far%d" % c], 8 * 8)
        g.dma_start(T.y[OFF[c]:OFF[c + 1], :], T["lf%d" % c][:], accum_op=AluOpType.add,
                    max_dma_last_dim=8192).then_inc(sem.done, 16)
    g.wait_ge(sem.done, 16 * K)
    g.wait_ge(sem.sent, n_sent)
